import numpy as np
import ml_dtypes


def mxq(x, axis, fmt="e4m3"):
    dtype, down = {"e4m3": (ml_dtypes.float8_e4m3fn, 7), "e5m2": (ml_dtypes.float8_e5m2, 14)}[fmt]
    v = np.moveaxis(np.asarray(x, np.float32).astype(ml_dtypes.bfloat16).astype(np.float64), axis, -1)
    blocks = v.reshape(v.shape[:-1] + (-1, 32))
    amax = np.abs(blocks).max(-1, keepdims=True)
    byte = np.maximum(np.where(amax > 0, np.frexp(amax)[1] - 1 + 127, 0) - down, 1)
    scale = np.exp2(byte - 127.0)
    codes = (blocks / scale).astype(np.float32).astype(dtype).astype(np.float64)
    return np.moveaxis((codes * scale).reshape(v.shape), -1, axis)


WIDE = False


def mx_kscale(k):
    if not WIDE:
        return np.ones(k)
    levels = np.array([10, -10, 5, -5, 0])
    if k % 512:
        return np.exp2(np.random.permutation(np.resize(levels, k // 32))).repeat(32)
    a = np.empty((k // 512, 16))
    for p in range(k // 512):
        a[p, :8] = np.random.permutation(np.resize(levels, 8))
        for g in range(8):
            far = levels[np.abs(levels - a[p, g]) >= 10]
            a[p, g + 8] = far[np.random.randint(len(far))]
    return np.exp2(a.ravel()).repeat(32)


def f64(x):
    return np.asarray(x).astype(np.float64)


E2M1 = np.array([0.0, 0.5, 1.0, 1.5, 2.0, 3.0, 4.0, 6.0, -0.0, -0.5, -1.0, -1.5, -2.0, -3.0, -4.0, -6.0])


def pack_weight(w, fmt):
    k, n = w.shape
    w = f64(np.asarray(w, np.float32).astype(ml_dtypes.bfloat16)).reshape(k // 32, 32, n)
    amax = np.abs(w).max(1)
    if fmt == "e4m3":
        byte = np.frexp(amax)[1] - 1 + 127 - 7
    else:
        mant, ex = np.frexp(amax / 6.0)
        byte = np.where(mant > 0.5, ex, ex - 1) + 127
    byte = np.clip(np.where(amax > 0, byte, 1), 1, 254)
    scaled = (w * np.exp2(127.0 - byte)[:, None, :]).reshape(k, n).astype(np.float32)
    by_word = np.ascontiguousarray(scaled.reshape(k // 512, 128, 4, n).transpose(0, 1, 3, 2))
    if fmt == "e4m3":
        words = by_word.astype(ml_dtypes.float8_e4m3fn).view(np.uint8)
    else:
        c = by_word.astype(ml_dtypes.float4_e2m1fn).view(np.uint8) & 0xF
        words = (c[..., 0::2] | (c[..., 1::2] << 4)).reshape(k // 512, 128, 2 * n)
    return np.ascontiguousarray(words), np.ascontiguousarray(byte.astype(np.uint8).reshape(k // 512, 16, n))


def unpack_weight(words, scales, fmt):
    g, _, n = scales.shape
    words = np.ascontiguousarray(words).reshape(g, 128, n, -1)
    if fmt == "e4m3":
        vals = words.view(ml_dtypes.float8_e4m3fn).astype(np.float64)
    else:
        nib = np.empty((g, 128, n, 4), np.uint8)
        nib[..., 0::2] = words & 0xF
        nib[..., 1::2] = words >> 4
        vals = E2M1[nib]
    vals = vals * np.repeat(np.exp2(scales.astype(np.float64) - 127.0), 8, axis=1)[..., None]
    return vals.transpose(0, 1, 3, 2).reshape(g * 512, n)


K, L, T, N = 1024, 512, 512, 512


def setup_inputs():
    n = np.random.standard_normal
    fk = mx_kscale(K)
    fl = mx_kscale(L)
    xtp = pack_weight(n((K, T)) * np.random.uniform(0.3, 1.7, (1, T)) / fk[:, None], "e4m3")
    xsp = pack_weight(n((L, T)) * np.random.uniform(0.3, 1.7, (1, T)) / fl[:, None], "e2m1")
    wsp = pack_weight(n((L, N)) * 1 / np.sqrt(L) * fl[:, None], "e4m3")
    wcp = pack_weight(n((K, N)) * 1 / np.sqrt(K) * fk[:, None], "e2m1")
    return {
        "xt_words": xtp[0],
        "xt_scales": xtp[1],
        "wa": (n((K, N)) * 1 / np.sqrt(K) * fk[:, None]).astype(np.float32),
        "xs_words": xsp[0],
        "xs_scales": xsp[1],
        "ws_words": wsp[0],
        "ws_scales": wsp[1],
        "wc_words": wcp[0],
        "wc_scales": wcp[1],
        "gm": (np.random.uniform(0.5, 2.0, (1, N))).astype(np.float32),
    }


def reference(xt_words, xt_scales, wa, xs_words, xs_scales, ws_words, ws_scales, wc_words, wc_scales, gm):
    xtu = unpack_weight(xt_words, xt_scales, "e4m3")
    xsu = unpack_weight(xs_words, xs_scales, "e2m1")
    wsu = unpack_weight(ws_words, ws_scales, "e4m3")
    wcu = unpack_weight(wc_words, wc_scales, "e2m1")
    waq = mxq(f64(wa), 0, "e4m3")
    a = xtu.T @ waq + xsu.T @ wsu
    b = xtu.T @ wcu
    ea = np.mean(np.square(a), axis=1, keepdims=True)
    eb = np.mean(np.square(b), axis=1, keepdims=True)
    y = (ea * a + eb * b) / (ea + eb + 0.01) * f64(gm)
    return y

@@ -1,0 +1,205 @@
+from contextlib import ExitStack
+
+import concourse.mybir as mybir
+from concourse.masks import make_identity
+
+K, L, T, N = 1024, 512, 512, 512
+FLOPS = 2 * T * N * (2 * K + L)
+
+F32 = mybir.dt.float32
+BF16 = mybir.dt.bfloat16
+I32 = mybir.dt.int32
+U32 = mybir.dt.uint32
+U8 = mybir.dt.uint8
+FP8X4 = mybir.dt.float8_e4m3fn_x4
+FP4X4 = mybir.dt.float4_e2m1fn_x4
+ALU = mybir.AluOpType
+ACT = mybir.ActivationFunctionType
+
+P = 128
+PACK = 4
+TILES = T // P
+EPS = 0.01
+WA_CHUNKS = [(0, 0, 256), (0, 256, 256), (1, 0, 256), (1, 256, 128), (1, 384, 128)]
+
+
+def tile_mix_rows_mixed_by_their_energy_kernel(
+    tc, xt_words, xt_scales, wa, xs_words, xs_scales, ws_words, ws_scales, wc_words, wc_scales, gm, out
+):
+    nc = tc.nc
+    with ExitStack() as ctx:
+        sb = ctx.enter_context(tc.tile_pool(name="sb", bufs=1))
+        ps = ctx.enter_context(tc.psum_pool(name="ps", bufs=1))
+        ctx.enter_context(tc.manual_schedule())
+
+        xt_plane = sb.tile([P, 2, T], U8, align_bytes=64)
+        wc_plane = sb.tile([P, 2, N], U8, align_bytes=64)
+        ws_plane = sb.tile([P, 1, N], U8, align_bytes=64)
+        xs_plane = sb.tile([P, 1, T], U8, align_bytes=64)
+        nc.gpsimd.memset(xt_plane[:].bitcast(I32), 0)
+        for plane in (wc_plane, xs_plane, ws_plane):
+            nc.vector.memset(plane[:].bitcast(I32), 0)
+
+        gm_rows = sb.tile([P, PACK], F32)
+        nc.gpsimd.dma_start(out=gm_rows[:], in_=gm.rearrange("o (p c) -> (o p) c", c=PACK))
+        ident = sb.tile([P, P], F32)
+        make_identity(nc, ident[:])
+
+        xt = sb.tile([P, 2, T], U32, align_bytes=64)
+        wc = sb.tile([P, 2, 2 * N], U8, align_bytes=64)
+        xs = sb.tile([P, 2 * T], U8, align_bytes=64)
+        ws = sb.tile([P, N], U32, align_bytes=64)
+
+        def load_scales(queue, plane, scales):
+            for r in range(4):
+                queue.dma_start(
+                    out=plane[r:P:32, :, :].bitcast(I32),
+                    in_=scales[:, r:16:4, :].rearrange("z q c -> q z c").bitcast(I32),
+                )
+
+        raw = []
+
+        def load_wa(i):
+            z, c0, w = WA_CHUNKS[i]
+            r = sb.tile([P, PACK, w], F32, name="raw%d" % i)
+            nc.sync.dma_start(
+                out=r[:], in_=wa[512 * z : 512 * (z + 1), c0 : c0 + w].rearrange("(p j) c -> p j c", j=PACK)
+            )
+            raw.append(r)
+
+        nc.sync.dma_start(out=xt[:].bitcast(I32), in_=xt_words.rearrange("z p c r -> p z (c r)").bitcast(I32))
+        load_scales(nc.sync, xt_plane, xt_scales)
+        nc.sync.dma_start(out=wc[:].bitcast(I32), in_=wc_words.rearrange("z p c -> p z c").bitcast(I32))
+        load_wa(0)
+        load_scales(nc.sync, wc_plane, wc_scales)
+        load_scales(nc.gpsimd, xs_plane, xs_scales)
+        load_wa(1)
+        load_wa(2)
+        load_scales(nc.sync, ws_plane, ws_scales)
+        load_wa(3)
+        load_wa(4)
+        nc.sync.dma_start(out=ws[:].bitcast(I32), in_=ws_words[0].rearrange("p c r -> p (c r)").bitcast(I32))
+        nc.sync.dma_start(out=xs[:].bitcast(I32), in_=xs_words[0].bitcast(I32))
+
+        xt_sc = [xt_plane[:, z, :] for z in range(2)]
+        ws_sc = ws_plane[:, 0, :]
+        wc_sc = [wc_plane[:, z, :] for z in range(2)]
+        xs_sc = xs_plane[:, 0, :]
+
+        gm_ps = ps.tile([P, PACK, P], F32, tag="a3")
+        for c in range(PACK):
+            nc.tensor.transpose(gm_ps[:, c, :], gm_rows[:, c : c + 1].to_broadcast([P, P]), ident[:])
+        gm_all = sb.tile([P, N], F32)
+        nc.scalar.copy(out=gm_all[:].rearrange("p (m c) -> p m c", c=PACK), in_=gm_ps[:].rearrange("p c m -> p m c"))
+
+        eb = sb.tile([P, TILES], F32)
+        ebe = sb.tile([P, TILES], F32)
+        ea = sb.tile([P, TILES], F32)
+        den = sb.tile([P, TILES], F32)
+        inv = sb.tile([P, TILES], F32)
+        root = N**-0.5
+
+        b_ps = []
+        for j in range(TILES):
+            tok = slice(j * P, (j + 1) * P)
+            bank = ps.tile([P, N], F32, name="b%d" % j, tag="b%d" % j)
+            for z in range(2):
+                nc.tensor.matmul_mx(
+                    out=bank[:],
+                    lhsT=xt[:, z, tok].bitcast(FP8X4),
+                    lhsT_scale=xt_sc[z][:, tok],
+                    rhs=wc[:, z, :].bitcast(FP4X4),
+                    rhs_scale=wc_sc[z],
+                    start=(z == 0),
+                    stop=(z == 1),
+                )
+            b_ps.append(bank)
+        be = []
+        for j in range(TILES):
+            sq = sb.tile([P, N], F32, name="sq", bufs=2)
+            nc.scalar.activation(out=sq[:], in_=b_ps[j][:], func=ACT.Square, scale=root, accum_out=eb[:, j : j + 1])
+            if j > 0:
+                t = sb.tile([P, N], F32, name="be%d" % (j - 1))
+                nc.scalar.activation(out=t[:], in_=b_ps[j - 1][:], func=ACT.Copy, scale=eb[:, j - 1 : j])
+                be.append(t)
+        t = sb.tile([P, N], F32, name="be3")
+        nc.scalar.activation(out=t[:], in_=b_ps[3][:], func=ACT.Copy, scale=eb[:, 3:4])
+        be.append(t)
+
+        a_ps = [ps.tile([P, N], F32, name="a%d" % j, tag="a%d" % j) for j in range(TILES)]
+
+        def cast(i):
+            w = WA_CHUNKS[i][2]
+            g = sb.tile([P, w, PACK], BF16, name="grouped%d" % i, align_bytes=64)
+            nc.vector.tensor_copy(
+                out=g[:].rearrange("p (c i) t -> p c t i", i=4), in_=raw[i][:].rearrange("p t (c i) -> p c t i", i=4)
+            )
+            return g
+
+        def quantize(i, g):
+            w = WA_CHUNKS[i][2]
+            codes = sb.tile([P, w], U32, name="codes%d" % i, align_bytes=64)
+            scales = sb.tile([P, w], U8, name="scales%d" % i, align_bytes=64)
+            nc.vector.quantize_mx(
+                out=codes[:].bitcast(FP8X4), scales=scales[:], in_=g[:].rearrange("p w j -> p (w j)")
+            )
+            return codes, scales
+
+        def wa_pass(i, j, q):
+            z, c0, w = WA_CHUNKS[i]
+            tok = slice(j * P, (j + 1) * P)
+            nc.tensor.matmul_mx(
+                out=a_ps[j][:, c0 : c0 + w],
+                lhsT=xt[:, z, tok].bitcast(FP8X4),
+                lhsT_scale=xt_sc[z][:, tok],
+                rhs=q[0][:].bitcast(FP8X4),
+                rhs_scale=q[1][:],
+                start=(i == 0),
+                stop=False,
+            )
+
+        last = len(WA_CHUNKS) - 1
+        for i in range(last + 1):
+            q = quantize(i, cast(i))
+            if i == last:
+                nc.vector.tensor_scalar(out=ebe[:], in0=eb[:], scalar1=EPS, scalar2=None, op0=ALU.add)
+            for j in range(TILES):
+                wa_pass(i, j, q)
+                if i == last:
+                    nc.tensor.matmul_mx(
+                        out=a_ps[j][:],
+                        lhsT=xs[:, 2 * j * P : 2 * (j + 1) * P].bitcast(FP4X4),
+                        lhsT_scale=xs_sc[:, j * P : (j + 1) * P],
+                        rhs=ws[:].bitcast(FP8X4),
+                        rhs_scale=ws_sc,
+                        start=False,
+                        stop=True,
+                    )
+
+        for j in range(TILES):
+            col = slice(j, j + 1)
+            sq = sb.tile([P, N], F32, name="sq", bufs=2)
+            nc.scalar.activation(out=sq[:], in_=a_ps[j][:], func=ACT.Square, scale=root, accum_out=ea[:, col])
+            nc.scalar.activation(out=den[:, col], in_=ea[:, col], func=ACT.Identity, bias=ebe[:, col])
+
+        mixed = []
+
+        def mix(j):
+            col = slice(j, j + 1)
+            u = sb.tile([P, N], F32, name="mixed%d" % j)
+            nc.vector.scalar_tensor_tensor(
+                out=u[:], in0=a_ps[j][:], scalar=ea[:, col], in1=be[j][:], op0=ALU.mult, op1=ALU.add
+            )
+            nc.vector.reciprocal(out=inv[:, col], in_=den[:, col])
+            mixed.append(u)
+
+        def finish(j):
+            y = sb.tile([P, N], F32, name="y%d" % j)
+            nc.vector.scalar_tensor_tensor(
+                out=y[:], in0=mixed[j][:], scalar=inv[:, j : j + 1], in1=gm_all[:], op0=ALU.mult, op1=ALU.mult
+            )
+            nc.sync.dma_start(out=out[j * P : (j + 1) * P, :], in_=y[:])
+
+        for j in range(TILES):
+            mix(j)
+            finish(j)

@@ -20,7 +20,7 @@ P = 128
 PACK = 4
 TILES = T // P
 EPS = 0.01
-WA_CHUNKS = [(0, 0, 256), (0, 256, 256), (1, 0, 256), (1, 256, 128), (1, 384, 128)]
+WA_CHUNKS = [(0, 0, 128), (0, 128, 128), (0, 256, 256), (1, 0, 256), (1, 256, 128), (1, 384, 128)]
 
 
 def tile_mix_rows_mixed_by_their_energy_kernel(
@@ -36,12 +36,10 @@ def tile_mix_rows_mixed_by_their_energy_kernel(
         wc_plane = sb.tile([P, 2, N], U8, align_bytes=64)
         ws_plane = sb.tile([P, 1, N], U8, align_bytes=64)
         xs_plane = sb.tile([P, 1, T], U8, align_bytes=64)
-        nc.gpsimd.memset(xt_plane[:].bitcast(I32), 0)
-        for plane in (wc_plane, xs_plane, ws_plane):
+        for plane in (xt_plane, wc_plane, xs_plane, ws_plane):
             nc.vector.memset(plane[:].bitcast(I32), 0)
 
         gm_rows = sb.tile([P, PACK], F32)
-        nc.gpsimd.dma_start(out=gm_rows[:], in_=gm.rearrange("o (p c) -> (o p) c", c=PACK))
         ident = sb.tile([P, P], F32)
         make_identity(nc, ident[:])
 
@@ -50,11 +48,11 @@ def tile_mix_rows_mixed_by_their_energy_kernel(
         xs = sb.tile([P, 2 * T], U8, align_bytes=64)
         ws = sb.tile([P, N], U32, align_bytes=64)
 
-        def load_scales(queue, plane, scales):
-            for r in range(4):
+        def load_scales(queue, plane, scales, quadrants=range(4)):
+            for q in quadrants:
                 queue.dma_start(
-                    out=plane[r:P:32, :, :].bitcast(I32),
-                    in_=scales[:, r:16:4, :].rearrange("z q c -> q z c").bitcast(I32),
+                    out=plane[32 * q : 32 * q + 4, :, :].bitcast(I32),
+                    in_=scales[:, 4 * q : 4 * q + 4, :].rearrange("z r c -> r z c").bitcast(I32),
                 )
 
         raw = []
@@ -67,19 +65,22 @@ def tile_mix_rows_mixed_by_their_energy_kernel(
             )
             raw.append(r)
 
-        nc.sync.dma_start(out=xt[:].bitcast(I32), in_=xt_words.rearrange("z p c r -> p z (c r)").bitcast(I32))
-        load_scales(nc.sync, xt_plane, xt_scales)
         nc.sync.dma_start(out=wc[:].bitcast(I32), in_=wc_words.rearrange("z p c -> p z c").bitcast(I32))
+        load_scales(nc.sync, xt_plane, xt_scales)
+        nc.sync.dma_start(out=gm_rows[:], in_=gm.rearrange("o (p c) -> (o p) c", c=PACK))
+        nc.sync.dma_start(out=xt[:].bitcast(I32), in_=xt_words.rearrange("z p c r -> p z (c r)").bitcast(I32))
         load_wa(0)
         load_scales(nc.sync, wc_plane, wc_scales)
         load_scales(nc.gpsimd, xs_plane, xs_scales)
         load_wa(1)
         load_wa(2)
-        load_scales(nc.sync, ws_plane, ws_scales)
+        load_scales(nc.sync, ws_plane, ws_scales, range(1))
         load_wa(3)
         load_wa(4)
-        nc.sync.dma_start(out=ws[:].bitcast(I32), in_=ws_words[0].rearrange("p c r -> p (c r)").bitcast(I32))
         nc.sync.dma_start(out=xs[:].bitcast(I32), in_=xs_words[0].bitcast(I32))
+        load_wa(5)
+        load_scales(nc.sync, ws_plane, ws_scales, range(1, 4))
+        nc.sync.dma_start(out=ws[:].bitcast(I32), in_=ws_words[0].rearrange("p c r -> p (c r)").bitcast(I32))
 
         xt_sc = [xt_plane[:, z, :] for z in range(2)]
         ws_sc = ws_plane[:, 0, :]
@@ -91,6 +92,18 @@ def tile_mix_rows_mixed_by_their_energy_kernel(
             nc.tensor.transpose(gm_ps[:, c, :], gm_rows[:, c : c + 1].to_broadcast([P, P]), ident[:])
         gm_all = sb.tile([P, N], F32)
         nc.scalar.copy(out=gm_all[:].rearrange("p (m c) -> p m c", c=PACK), in_=gm_ps[:].rearrange("p c m -> p m c"))
+
+        warm = ps.tile([P, N], F32, tag="a0")
+        for rep in range(2):
+            nc.tensor.matmul_mx(
+                out=warm[:],
+                lhsT=xt[:, 0, 0:P].bitcast(FP8X4),
+                lhsT_scale=xt_sc[0][:, 0:P],
+                rhs=xt[:, 0, :].bitcast(FP8X4),
+                rhs_scale=xt_sc[0],
+                start=True,
+                stop=True,
+            )
 
         eb = sb.tile([P, TILES], F32)
         ebe = sb.tile([P, TILES], F32)
@@ -114,92 +127,149 @@ def tile_mix_rows_mixed_by_their_energy_kernel(
                     stop=(z == 1),
                 )
             b_ps.append(bank)
-        be = []
-        for j in range(TILES):
+        be = {}
+
+        def energy(bank, total, cols=slice(0, N)):
             sq = sb.tile([P, N], F32, name="sq", bufs=2)
-            nc.scalar.activation(out=sq[:], in_=b_ps[j][:], func=ACT.Square, scale=root, accum_out=eb[:, j : j + 1])
-            if j > 0:
-                t = sb.tile([P, N], F32, name="be%d" % (j - 1))
-                nc.scalar.activation(out=t[:], in_=b_ps[j - 1][:], func=ACT.Copy, scale=eb[:, j - 1 : j])
-                be.append(t)
-        t = sb.tile([P, N], F32, name="be3")
-        nc.scalar.activation(out=t[:], in_=b_ps[3][:], func=ACT.Copy, scale=eb[:, 3:4])
-        be.append(t)
+            nc.scalar.activation(out=sq[:, cols], in_=bank[:, cols], func=ACT.Square, scale=root, accum_out=total)
+
+        def weigh_b(j):
+            be[j] = sb.tile([P, N], F32, name="be%d" % j)
+            nc.scalar.activation(out=be[j][:], in_=b_ps[j][:], func=ACT.Copy, scale=eb[:, j : j + 1])
+
+        def floor_b(cols):
+            nc.scalar.activation(out=ebe[:, cols], in_=eb[:, cols], func=ACT.Copy, bias=EPS)
+
+        for j in range(TILES):
+            energy(b_ps[j], eb[:, j : j + 1])
+            if j > 1:
+                weigh_b(j - 1)
+        floor_b(slice(0, TILES))
+        weigh_b(TILES - 1)
 
         a_ps = [ps.tile([P, N], F32, name="a%d" % j, tag="a%d" % j) for j in range(TILES)]
+        a0_right = ps.tile([P, N], F32, tag="b1")
+        wa_codes = [sb.tile([P, N], U32, name="wa_codes%d" % z, align_bytes=64) for z in range(2)]
+        wa_plane = [sb.tile([P, N], U8, name="wa_plane%d" % z, align_bytes=64) for z in range(2)]
+
+        grouped = []
 
         def cast(i):
-            w = WA_CHUNKS[i][2]
-            g = sb.tile([P, w, PACK], BF16, name="grouped%d" % i, align_bytes=64)
+            g = sb.tile([P, WA_CHUNKS[i][2], PACK], BF16, name="grouped%d" % i, align_bytes=64)
             nc.vector.tensor_copy(
                 out=g[:].rearrange("p (c i) t -> p c t i", i=4), in_=raw[i][:].rearrange("p t (c i) -> p c t i", i=4)
             )
-            return g
+            grouped.append(g)
 
-        def quantize(i, g):
-            w = WA_CHUNKS[i][2]
-            codes = sb.tile([P, w], U32, name="codes%d" % i, align_bytes=64)
-            scales = sb.tile([P, w], U8, name="scales%d" % i, align_bytes=64)
-            nc.vector.quantize_mx(
-                out=codes[:].bitcast(FP8X4), scales=scales[:], in_=g[:].rearrange("p w j -> p (w j)")
-            )
-            return codes, scales
-
-        def wa_pass(i, j, q):
+        def quantize(i):
             z, c0, w = WA_CHUNKS[i]
+            for lo in range(0, w, 256):
+                hi = min(lo + 256, w)
+                nc.vector.quantize_mx(
+                    out=wa_codes[z][:, c0 + lo : c0 + hi].bitcast(FP8X4),
+                    scales=wa_plane[z][:, c0 + lo : c0 + hi],
+                    in_=grouped[i][:, lo:hi, :].rearrange("p w j -> p (w j)"),
+                )
+
+        for i in range(3):
+            cast(i)
+            quantize(i)
+        cast(3)
+        for i in range(4, len(WA_CHUNKS)):
+            cast(i)
+            quantize(i - 1)
+        quantize(len(WA_CHUNKS) - 1)
+
+        def wa_pass(bank, z, j, cols, stop=False):
             tok = slice(j * P, (j + 1) * P)
             nc.tensor.matmul_mx(
-                out=a_ps[j][:, c0 : c0 + w],
+                out=bank[:, cols],
                 lhsT=xt[:, z, tok].bitcast(FP8X4),
                 lhsT_scale=xt_sc[z][:, tok],
-                rhs=q[0][:].bitcast(FP8X4),
-                rhs_scale=q[1][:],
-                start=(i == 0),
-                stop=False,
+                rhs=wa_codes[z][:, cols].bitcast(FP8X4),
+                rhs_scale=wa_plane[z][:, cols],
+                start=(z == 0),
+                stop=stop,
             )
 
-        last = len(WA_CHUNKS) - 1
-        for i in range(last + 1):
-            q = quantize(i, cast(i))
-            if i == last:
-                nc.vector.tensor_scalar(out=ebe[:], in0=eb[:], scalar1=EPS, scalar2=None, op0=ALU.add)
-            for j in range(TILES):
-                wa_pass(i, j, q)
-                if i == last:
-                    nc.tensor.matmul_mx(
-                        out=a_ps[j][:],
-                        lhsT=xs[:, 2 * j * P : 2 * (j + 1) * P].bitcast(FP4X4),
-                        lhsT_scale=xs_sc[:, j * P : (j + 1) * P],
-                        rhs=ws[:].bitcast(FP8X4),
-                        rhs_scale=ws_sc,
-                        start=False,
-                        stop=True,
-                    )
+        def ws_pass(bank, j, cols, stop):
+            nc.tensor.matmul_mx(
+                out=bank[:, cols],
+                lhsT=xs[:, 2 * j * P : 2 * (j + 1) * P].bitcast(FP4X4),
+                lhsT_scale=xs_sc[:, j * P : (j + 1) * P],
+                rhs=ws[:, cols].bitcast(FP8X4),
+                rhs_scale=ws_sc[:, cols],
+                start=False,
+                stop=stop,
+            )
 
-        for j in range(TILES):
+        left, right, whole = slice(0, N // 2), slice(N // 2, N), slice(0, N)
+        quarter = [slice(q * P, (q + 1) * P) for q in range(4)]
+        wa_pass(a_ps[0], 0, 0, left)
+        for j in range(1, TILES):
+            wa_pass(a_ps[j], 0, j, whole)
+        wa_pass(a0_right, 0, 0, right)
+        wa_pass(a_ps[0], 1, 0, left)
+        wa_pass(a0_right, 1, 0, quarter[2])
+        ws_pass(a_ps[0], 0, quarter[0], False)
+        ws_pass(a_ps[0], 0, quarter[1], True)
+        ws_pass(a0_right, 0, quarter[2], False)
+        ws_pass(a0_right, 0, quarter[3], False)
+        wa_pass(a0_right, 1, 0, quarter[3], True)
+        for j in range(1, TILES):
+            wa_pass(a_ps[j], 1, j, whole)
+            ws_pass(a_ps[j], j, whole, True)
+
+        halves = sb.tile([P, 2], F32)
+        bg = sb.tile([P, N], F32)
+        ag = sb.tile([P, N], F32)
+        v = sb.tile([P, N], F32)
+        nc.vector.scalar_tensor_tensor(
+            out=bg[:], in0=b_ps[0][:], scalar=eb[:, 0:1], in1=gm_all[:], op0=ALU.mult, op1=ALU.mult
+        )
+        energy(a_ps[0], halves[:, 0:1], left)
+        nc.vector.tensor_tensor(out=ag[:, right], in0=a0_right[:, right], in1=gm_all[:, right], op=ALU.mult)
+        energy(a0_right, halves[:, 1:2], right)
+        nc.vector.tensor_tensor(out=ag[:, left], in0=a_ps[0][:, left], in1=gm_all[:, left], op=ALU.mult)
+        nc.scalar.activation(out=ea[:, 0:1], in_=halves[:, 1:2], func=ACT.Identity, bias=halves[:, 0:1])
+        nc.vector.scalar_tensor_tensor(
+            out=v[:], in0=ag[:], scalar=ea[:, 0:1], in1=bg[:], op0=ALU.mult, op1=ALU.add
+        )
+
+        mixed = {}
+
+        def denominator(j):
             col = slice(j, j + 1)
-            sq = sb.tile([P, N], F32, name="sq", bufs=2)
-            nc.scalar.activation(out=sq[:], in_=a_ps[j][:], func=ACT.Square, scale=root, accum_out=ea[:, col])
             nc.scalar.activation(out=den[:, col], in_=ea[:, col], func=ACT.Identity, bias=ebe[:, col])
 
-        mixed = []
+        def invert(j):
+            nc.vector.reciprocal(out=inv[:, j : j + 1], in_=den[:, j : j + 1])
 
         def mix(j):
-            col = slice(j, j + 1)
-            u = sb.tile([P, N], F32, name="mixed%d" % j)
+            mixed[j] = sb.tile([P, N], F32, name="mixed%d" % j)
             nc.vector.scalar_tensor_tensor(
-                out=u[:], in0=a_ps[j][:], scalar=ea[:, col], in1=be[j][:], op0=ALU.mult, op1=ALU.add
+                out=mixed[j][:], in0=a_ps[j][:], scalar=ea[:, j : j + 1], in1=be[j][:], op0=ALU.mult, op1=ALU.add
             )
-            nc.vector.reciprocal(out=inv[:, col], in_=den[:, col])
-            mixed.append(u)
 
-        def finish(j):
-            y = sb.tile([P, N], F32, name="y%d" % j)
+        def finish(j, cols):
+            y = sb.tile([P, cols.stop - cols.start], F32, name="y%d_%d" % (j, cols.start))
             nc.vector.scalar_tensor_tensor(
-                out=y[:], in0=mixed[j][:], scalar=inv[:, j : j + 1], in1=gm_all[:], op0=ALU.mult, op1=ALU.mult
+                out=y[:], in0=mixed[j][:, cols], scalar=inv[:, j : j + 1], in1=gm_all[:, cols], op0=ALU.mult, op1=ALU.mult
             )
-            nc.sync.dma_start(out=out[j * P : (j + 1) * P, :], in_=y[:])
+            nc.sync.dma_start(out=out[j * P : (j + 1) * P, cols], in_=y[:])
 
-        for j in range(TILES):
+        for j in range(1, TILES):
+            energy(a_ps[j], ea[:, j : j + 1])
+            denominator(j - 1)
+            invert(j - 1)
             mix(j)
-            finish(j)
+            if j == TILES - 1:
+                y0 = sb.tile([P, N], F32)
+                nc.scalar.activation(out=y0[:], in_=v[:], func=ACT.Copy, scale=inv[:, 0:1])
+                nc.sync.dma_start(out=out[0:P, :], in_=y0[:])
+            if j > 1:
+                finish(j - 1, whole)
+        denominator(TILES - 1)
+        invert(TILES - 1)
+        finish(TILES - 1, left)
+        finish(TILES - 1, right)

@@ -48,11 +48,11 @@ def tile_mix_rows_mixed_by_their_energy_kernel(
         xs = sb.tile([P, 2 * T], U8, align_bytes=64)
         ws = sb.tile([P, N], U32, align_bytes=64)
 
-        def load_scales(queue, plane, scales, quadrants=range(4)):
-            for q in quadrants:
+        def load_scales(queue, plane, scales, rows=range(4)):
+            for r in rows:
                 queue.dma_start(
-                    out=plane[32 * q : 32 * q + 4, :, :].bitcast(I32),
-                    in_=scales[:, 4 * q : 4 * q + 4, :].rearrange("z r c -> r z c").bitcast(I32),
+                    out=plane[r:P:32, :, :].bitcast(I32),
+                    in_=scales[:, r:16:4, :].rearrange("z q c -> q z c").bitcast(I32),
                 )
 
         raw = []
@@ -145,7 +145,6 @@ def tile_mix_rows_mixed_by_their_energy_kernel(
             if j > 1:
                 weigh_b(j - 1)
         floor_b(slice(0, TILES))
-        weigh_b(TILES - 1)
 
         a_ps = [ps.tile([P, N], F32, name="a%d" % j, tag="a%d" % j) for j in range(TILES)]
         a0_right = ps.tile([P, N], F32, tag="b1")
@@ -220,21 +219,31 @@ def tile_mix_rows_mixed_by_their_energy_kernel(
             wa_pass(a_ps[j], 1, j, whole)
             ws_pass(a_ps[j], j, whole, True)
 
-        halves = sb.tile([P, 2], F32)
+        left_sums = sb.tile([P, 2], F32)
+        right_sum = sb.tile([P, 1], F32)
+        first = sb.tile([P, 2], F32)
         bg = sb.tile([P, N], F32)
         ag = sb.tile([P, N], F32)
         v = sb.tile([P, N], F32)
         nc.vector.scalar_tensor_tensor(
             out=bg[:], in0=b_ps[0][:], scalar=eb[:, 0:1], in1=gm_all[:], op0=ALU.mult, op1=ALU.mult
         )
-        energy(a_ps[0], halves[:, 0:1], left)
-        nc.vector.tensor_tensor(out=ag[:, right], in0=a0_right[:, right], in1=gm_all[:, right], op=ALU.mult)
-        energy(a0_right, halves[:, 1:2], right)
-        nc.vector.tensor_tensor(out=ag[:, left], in0=a_ps[0][:, left], in1=gm_all[:, left], op=ALU.mult)
-        nc.scalar.activation(out=ea[:, 0:1], in_=halves[:, 1:2], func=ACT.Identity, bias=halves[:, 0:1])
-        nc.vector.scalar_tensor_tensor(
-            out=v[:], in0=ag[:], scalar=ea[:, 0:1], in1=bg[:], op0=ALU.mult, op1=ALU.add
-        )
+        be[3] = sb.tile([P, N], F32, name="be3")
+        nc.vector.tensor_scalar(out=be[3][:], in0=b_ps[3][:], scalar1=eb[:, 3:4], scalar2=None, op0=ALU.mult)
+        energy(a_ps[0], left_sums[:, 0:1], left)
+        energy(a0_right, right_sum[:], right)
+        nc.scalar.activation(out=left_sums[:, 1:2], in_=left_sums[:, 0:1], func=ACT.Identity, bias=ebe[:, 0:1])
+        nc.scalar.activation(out=first[:], in_=left_sums[:], func=ACT.Identity, bias=right_sum[:])
+        for bank, cols in ((a_ps[0], left), (a0_right, right)):
+            nc.vector.tensor_tensor(out=ag[:, cols], in0=bank[:, cols], in1=gm_all[:, cols], op=ALU.mult)
+        for cols in (left, right):
+            nc.vector.scalar_tensor_tensor(
+                out=v[:, cols], in0=ag[:, cols], scalar=first[:, 0:1], in1=bg[:, cols], op0=ALU.mult, op1=ALU.add
+            )
+        nc.vector.reciprocal(out=inv[:, 0:1], in_=first[:, 1:2])
+        y0 = sb.tile([P, N], F32)
+        nc.gpsimd.tensor_scalar(out=y0[:], in0=v[:], scalar1=inv[:, 0:1], scalar2=0.0, op0=ALU.mult, op1=ALU.add)
+        nc.sync.dma_start(out=out[0:P, :], in_=y0[:])
 
         mixed = {}
 
@@ -260,16 +269,14 @@ def tile_mix_rows_mixed_by_their_energy_kernel(
 
         for j in range(1, TILES):
             energy(a_ps[j], ea[:, j : j + 1])
-            denominator(j - 1)
-            invert(j - 1)
+            if j > 1:
+                denominator(j - 1)
+                invert(j - 1)
             mix(j)
             if j == TILES - 1:
-                y0 = sb.tile([P, N], F32)
-                nc.scalar.activation(out=y0[:], in_=v[:], func=ACT.Copy, scale=inv[:, 0:1])
-                nc.sync.dma_start(out=out[0:P, :], in_=y0[:])
+                denominator(j)
+                invert(j)
             if j > 1:
                 finish(j - 1, whole)
-        denominator(TILES - 1)
-        invert(TILES - 1)
         finish(TILES - 1, left)
         finish(TILES - 1, right)

@@ -65,11 +65,11 @@ def tile_mix_rows_mixed_by_their_energy_kernel(
             )
             raw.append(r)
 
-        nc.sync.dma_start(out=wc[:].bitcast(I32), in_=wc_words.rearrange("z p c -> p z c").bitcast(I32))
+        load_wa(0)
         load_scales(nc.sync, xt_plane, xt_scales)
         nc.sync.dma_start(out=gm_rows[:], in_=gm.rearrange("o (p c) -> (o p) c", c=PACK))
         nc.sync.dma_start(out=xt[:].bitcast(I32), in_=xt_words.rearrange("z p c r -> p z (c r)").bitcast(I32))
-        load_wa(0)
+        nc.sync.dma_start(out=wc[:].bitcast(I32), in_=wc_words.rearrange("z p c -> p z c").bitcast(I32))
         load_scales(nc.sync, wc_plane, wc_scales)
         load_scales(nc.gpsimd, xs_plane, xs_scales)
         load_wa(1)
@@ -87,23 +87,51 @@ def tile_mix_rows_mixed_by_their_energy_kernel(
         wc_sc = [wc_plane[:, z, :] for z in range(2)]
         xs_sc = xs_plane[:, 0, :]
 
-        gm_ps = ps.tile([P, PACK, P], F32, tag="a3")
+        gm_ps = ps.tile([P, PACK, P], F32, tag="b3")
         for c in range(PACK):
             nc.tensor.transpose(gm_ps[:, c, :], gm_rows[:, c : c + 1].to_broadcast([P, P]), ident[:])
         gm_all = sb.tile([P, N], F32)
         nc.scalar.copy(out=gm_all[:].rearrange("p (m c) -> p m c", c=PACK), in_=gm_ps[:].rearrange("p c m -> p m c"))
 
-        warm = ps.tile([P, N], F32, tag="a0")
-        for rep in range(2):
-            nc.tensor.matmul_mx(
-                out=warm[:],
-                lhsT=xt[:, 0, 0:P].bitcast(FP8X4),
-                lhsT_scale=xt_sc[0][:, 0:P],
-                rhs=xt[:, 0, :].bitcast(FP8X4),
-                rhs_scale=xt_sc[0],
-                start=True,
-                stop=True,
+        a_ps = [ps.tile([P, N], F32, name="a%d" % j, tag="a%d" % j) for j in range(TILES)]
+        wa_codes = [sb.tile([P, N], U32, name="wa_codes%d" % z, align_bytes=64) for z in range(2)]
+        wa_plane = [sb.tile([P, N], U8, name="wa_plane%d" % z, align_bytes=64) for z in range(2)]
+
+        grouped = []
+
+        def cast(i):
+            g = sb.tile([P, WA_CHUNKS[i][2], PACK], BF16, name="grouped%d" % i, align_bytes=64)
+            nc.vector.tensor_copy(
+                out=g[:].rearrange("p (c i) t -> p c t i", i=4), in_=raw[i][:].rearrange("p t (c i) -> p c t i", i=4)
             )
+            grouped.append(g)
+
+        def quantize(i):
+            z, c0, w = WA_CHUNKS[i]
+            for lo in range(0, w, 256):
+                hi = min(lo + 256, w)
+                nc.vector.quantize_mx(
+                    out=wa_codes[z][:, c0 + lo : c0 + hi].bitcast(FP8X4),
+                    scales=wa_plane[z][:, c0 + lo : c0 + hi],
+                    in_=grouped[i][:, lo:hi, :].rearrange("p w j -> p (w j)"),
+                )
+
+        def wa_pass(bank, z, j, cols, start=False, stop=False):
+            tok = slice(j * P, (j + 1) * P)
+            nc.tensor.matmul_mx(
+                out=bank[:, cols],
+                lhsT=xt[:, z, tok].bitcast(FP8X4),
+                lhsT_scale=xt_sc[z][:, tok],
+                rhs=wa_codes[z][:, cols].bitcast(FP8X4),
+                rhs_scale=wa_plane[z][:, cols],
+                start=start,
+                stop=stop,
+            )
+
+        cast(0)
+        quantize(0)
+        for j in range(TILES):
+            wa_pass(a_ps[j], 0, j, slice(0, P), start=True)
 
         eb = sb.tile([P, TILES], F32)
         ebe = sb.tile([P, TILES], F32)
@@ -146,31 +174,8 @@ def tile_mix_rows_mixed_by_their_energy_kernel(
                 weigh_b(j - 1)
         floor_b(slice(0, TILES))
 
-        a_ps = [ps.tile([P, N], F32, name="a%d" % j, tag="a%d" % j) for j in range(TILES)]
         a0_right = ps.tile([P, N], F32, tag="b1")
-        wa_codes = [sb.tile([P, N], U32, name="wa_codes%d" % z, align_bytes=64) for z in range(2)]
-        wa_plane = [sb.tile([P, N], U8, name="wa_plane%d" % z, align_bytes=64) for z in range(2)]
-
-        grouped = []
-
-        def cast(i):
-            g = sb.tile([P, WA_CHUNKS[i][2], PACK], BF16, name="grouped%d" % i, align_bytes=64)
-            nc.vector.tensor_copy(
-                out=g[:].rearrange("p (c i) t -> p c t i", i=4), in_=raw[i][:].rearrange("p t (c i) -> p c t i", i=4)
-            )
-            grouped.append(g)
-
-        def quantize(i):
-            z, c0, w = WA_CHUNKS[i]
-            for lo in range(0, w, 256):
-                hi = min(lo + 256, w)
-                nc.vector.quantize_mx(
-                    out=wa_codes[z][:, c0 + lo : c0 + hi].bitcast(FP8X4),
-                    scales=wa_plane[z][:, c0 + lo : c0 + hi],
-                    in_=grouped[i][:, lo:hi, :].rearrange("p w j -> p (w j)"),
-                )
-
-        for i in range(3):
+        for i in range(1, 3):
             cast(i)
             quantize(i)
         cast(3)
@@ -178,18 +183,6 @@ def tile_mix_rows_mixed_by_their_energy_kernel(
             cast(i)
             quantize(i - 1)
         quantize(len(WA_CHUNKS) - 1)
-
-        def wa_pass(bank, z, j, cols, stop=False):
-            tok = slice(j * P, (j + 1) * P)
-            nc.tensor.matmul_mx(
-                out=bank[:, cols],
-                lhsT=xt[:, z, tok].bitcast(FP8X4),
-                lhsT_scale=xt_sc[z][:, tok],
-                rhs=wa_codes[z][:, cols].bitcast(FP8X4),
-                rhs_scale=wa_plane[z][:, cols],
-                start=(z == 0),
-                stop=stop,
-            )
 
         def ws_pass(bank, j, cols, stop):
             nc.tensor.matmul_mx(
@@ -204,17 +197,18 @@ def tile_mix_rows_mixed_by_their_energy_kernel(
 
         left, right, whole = slice(0, N // 2), slice(N // 2, N), slice(0, N)
         quarter = [slice(q * P, (q + 1) * P) for q in range(4)]
-        wa_pass(a_ps[0], 0, 0, left)
-        for j in range(1, TILES):
-            wa_pass(a_ps[j], 0, j, whole)
-        wa_pass(a0_right, 0, 0, right)
+        for j in range(TILES):
+            wa_pass(a_ps[j], 0, j, quarter[1])
+            if j > 0:
+                wa_pass(a_ps[j], 0, j, right)
+        wa_pass(a0_right, 0, 0, right, start=True)
         wa_pass(a_ps[0], 1, 0, left)
         wa_pass(a0_right, 1, 0, quarter[2])
         ws_pass(a_ps[0], 0, quarter[0], False)
         ws_pass(a_ps[0], 0, quarter[1], True)
         ws_pass(a0_right, 0, quarter[2], False)
         ws_pass(a0_right, 0, quarter[3], False)
-        wa_pass(a0_right, 1, 0, quarter[3], True)
+        wa_pass(a0_right, 1, 0, quarter[3], stop=True)
         for j in range(1, TILES):
             wa_pass(a_ps[j], 1, j, whole)
             ws_pass(a_ps[j], j, whole, True)

@@ -18,15 +18,22 @@ ACT = mybir.ActivationFunctionType
 
 P = 128
 PACK = 4
+K_PASS = P * PACK
 TILES = T // P
+LAST = TILES - 1
 EPS = 0.01
-WA_CHUNKS = [(0, 0, 128), (0, 128, 128), (0, 256, 256), (1, 0, 256), (1, 256, 128), (1, 384, 128)]
+SCALE_ROWS = 4
+WA_PIECES = [(0, 0, 128), (0, 128, 128), (0, 256, 256), (1, 0, 256), (1, 256, 128), (1, 384, 128)]
+WARM_PASSES = 6
 
 
 def tile_mix_rows_mixed_by_their_energy_kernel(
     tc, xt_words, xt_scales, wa, xs_words, xs_scales, ws_words, ws_scales, wc_words, wc_scales, gm, out
 ):
     nc = tc.nc
+    left, right, whole = slice(0, N // 2), slice(N // 2, N), slice(0, N)
+    quarter = [slice(q * P, (q + 1) * P) for q in range(N // P)]
+
     with ExitStack() as ctx:
         sb = ctx.enter_context(tc.tile_pool(name="sb", bufs=1))
         ps = ctx.enter_context(tc.psum_pool(name="ps", bufs=1))
@@ -48,22 +55,21 @@ def tile_mix_rows_mixed_by_their_energy_kernel(
         xs = sb.tile([P, 2 * T], U8, align_bytes=64)
         ws = sb.tile([P, N], U32, align_bytes=64)
 
-        def load_scales(queue, plane, scales, rows=range(4)):
+        def load_scales(queue, plane, scales, rows=range(SCALE_ROWS)):
             for r in rows:
                 queue.dma_start(
                     out=plane[r:P:32, :, :].bitcast(I32),
-                    in_=scales[:, r:16:4, :].rearrange("z q c -> q z c").bitcast(I32),
+                    in_=scales[:, r : 4 * SCALE_ROWS : SCALE_ROWS, :].rearrange("z q c -> q z c").bitcast(I32),
                 )
 
         raw = []
 
         def load_wa(i):
-            z, c0, w = WA_CHUNKS[i]
-            r = sb.tile([P, PACK, w], F32, name="raw%d" % i)
-            nc.sync.dma_start(
-                out=r[:], in_=wa[512 * z : 512 * (z + 1), c0 : c0 + w].rearrange("(p j) c -> p j c", j=PACK)
-            )
-            raw.append(r)
+            z, c0, w = WA_PIECES[i]
+            piece = sb.tile([P, PACK, w], F32, name="raw%d" % i)
+            rows = wa[K_PASS * z : K_PASS * (z + 1), c0 : c0 + w]
+            nc.sync.dma_start(out=piece[:], in_=rows.rearrange("(p j) c -> p j c", j=PACK))
+            raw.append(piece)
 
         load_wa(0)
         load_scales(nc.sync, xt_plane, xt_scales)
@@ -79,15 +85,10 @@ def tile_mix_rows_mixed_by_their_energy_kernel(
         load_wa(4)
         nc.sync.dma_start(out=xs[:].bitcast(I32), in_=xs_words[0].bitcast(I32))
         load_wa(5)
-        load_scales(nc.sync, ws_plane, ws_scales, range(1, 4))
+        load_scales(nc.sync, ws_plane, ws_scales, range(1, SCALE_ROWS))
         nc.sync.dma_start(out=ws[:].bitcast(I32), in_=ws_words[0].rearrange("p c r -> p (c r)").bitcast(I32))
 
-        xt_sc = [xt_plane[:, z, :] for z in range(2)]
-        ws_sc = ws_plane[:, 0, :]
-        wc_sc = [wc_plane[:, z, :] for z in range(2)]
-        xs_sc = xs_plane[:, 0, :]
-
-        gm_ps = ps.tile([P, PACK, P], F32, tag="b3")
+        gm_ps = ps.tile([P, PACK, P], F32, tag="b%d" % LAST)
         for c in range(PACK):
             nc.tensor.transpose(gm_ps[:, c, :], gm_rows[:, c : c + 1].to_broadcast([P, P]), ident[:])
         gm_all = sb.tile([P, N], F32)
@@ -96,181 +97,194 @@ def tile_mix_rows_mixed_by_their_energy_kernel(
         a_ps = [ps.tile([P, N], F32, name="a%d" % j, tag="a%d" % j) for j in range(TILES)]
         wa_codes = [sb.tile([P, N], U32, name="wa_codes%d" % z, align_bytes=64) for z in range(2)]
         wa_plane = [sb.tile([P, N], U8, name="wa_plane%d" % z, align_bytes=64) for z in range(2)]
-
         grouped = []
 
         def cast(i):
-            g = sb.tile([P, WA_CHUNKS[i][2], PACK], BF16, name="grouped%d" % i, align_bytes=64)
+            piece = sb.tile([P, WA_PIECES[i][2], PACK], BF16, name="grouped%d" % i, align_bytes=64)
             nc.vector.tensor_copy(
-                out=g[:].rearrange("p (c i) t -> p c t i", i=4), in_=raw[i][:].rearrange("p t (c i) -> p c t i", i=4)
+                out=piece[:].rearrange("p (c i) j -> p c j i", i=4),
+                in_=raw[i][:].rearrange("p j (c i) -> p c j i", i=4),
             )
-            grouped.append(g)
+            grouped.append(piece)
 
         def quantize(i):
-            z, c0, w = WA_CHUNKS[i]
-            for lo in range(0, w, 256):
-                hi = min(lo + 256, w)
-                nc.vector.quantize_mx(
-                    out=wa_codes[z][:, c0 + lo : c0 + hi].bitcast(FP8X4),
-                    scales=wa_plane[z][:, c0 + lo : c0 + hi],
-                    in_=grouped[i][:, lo:hi, :].rearrange("p w j -> p (w j)"),
-                )
+            z, c0, w = WA_PIECES[i]
+            nc.vector.quantize_mx(
+                out=wa_codes[z][:, c0 : c0 + w].bitcast(FP8X4),
+                scales=wa_plane[z][:, c0 : c0 + w],
+                in_=grouped[i][:].rearrange("p w j -> p (w j)"),
+            )
 
         def wa_pass(bank, z, j, cols, start=False, stop=False):
-            tok = slice(j * P, (j + 1) * P)
+            tokens = slice(j * P, (j + 1) * P)
             nc.tensor.matmul_mx(
                 out=bank[:, cols],
-                lhsT=xt[:, z, tok].bitcast(FP8X4),
-                lhsT_scale=xt_sc[z][:, tok],
+                lhsT=xt[:, z, tokens].bitcast(FP8X4),
+                lhsT_scale=xt_plane[:, z, tokens],
                 rhs=wa_codes[z][:, cols].bitcast(FP8X4),
                 rhs_scale=wa_plane[z][:, cols],
                 start=start,
                 stop=stop,
             )
 
-        cast(0)
-        quantize(0)
-        for j in range(TILES):
-            wa_pass(a_ps[j], 0, j, slice(0, P), start=True)
-
-        eb = sb.tile([P, TILES], F32)
-        ebe = sb.tile([P, TILES], F32)
-        ea = sb.tile([P, TILES], F32)
-        den = sb.tile([P, TILES], F32)
-        inv = sb.tile([P, TILES], F32)
-        root = N**-0.5
-
-        b_ps = []
-        for j in range(TILES):
-            tok = slice(j * P, (j + 1) * P)
-            bank = ps.tile([P, N], F32, name="b%d" % j, tag="b%d" % j)
-            for z in range(2):
-                nc.tensor.matmul_mx(
-                    out=bank[:],
-                    lhsT=xt[:, z, tok].bitcast(FP8X4),
-                    lhsT_scale=xt_sc[z][:, tok],
-                    rhs=wc[:, z, :].bitcast(FP4X4),
-                    rhs_scale=wc_sc[z],
-                    start=(z == 0),
-                    stop=(z == 1),
-                )
-            b_ps.append(bank)
-        be = {}
-
-        def energy(bank, total, cols=slice(0, N)):
-            sq = sb.tile([P, N], F32, name="sq", bufs=2)
-            nc.scalar.activation(out=sq[:, cols], in_=bank[:, cols], func=ACT.Square, scale=root, accum_out=total)
-
-        def weigh_b(j):
-            be[j] = sb.tile([P, N], F32, name="be%d" % j)
-            nc.scalar.activation(out=be[j][:], in_=b_ps[j][:], func=ACT.Copy, scale=eb[:, j : j + 1])
-
-        def floor_b(cols):
-            nc.scalar.activation(out=ebe[:, cols], in_=eb[:, cols], func=ACT.Copy, bias=EPS)
-
-        for j in range(TILES):
-            energy(b_ps[j], eb[:, j : j + 1])
-            if j > 1:
-                weigh_b(j - 1)
-        floor_b(slice(0, TILES))
-
-        a0_right = ps.tile([P, N], F32, tag="b1")
-        for i in range(1, 3):
-            cast(i)
-            quantize(i)
-        cast(3)
-        for i in range(4, len(WA_CHUNKS)):
-            cast(i)
-            quantize(i - 1)
-        quantize(len(WA_CHUNKS) - 1)
-
-        def ws_pass(bank, j, cols, stop):
+        def ws_pass(bank, j, cols, stop=False):
             nc.tensor.matmul_mx(
                 out=bank[:, cols],
                 lhsT=xs[:, 2 * j * P : 2 * (j + 1) * P].bitcast(FP4X4),
-                lhsT_scale=xs_sc[:, j * P : (j + 1) * P],
+                lhsT_scale=xs_plane[:, 0, j * P : (j + 1) * P],
                 rhs=ws[:, cols].bitcast(FP8X4),
-                rhs_scale=ws_sc[:, cols],
+                rhs_scale=ws_plane[:, 0, cols],
                 start=False,
                 stop=stop,
             )
 
-        left, right, whole = slice(0, N // 2), slice(N // 2, N), slice(0, N)
-        quarter = [slice(q * P, (q + 1) * P) for q in range(4)]
+        cast(0)
+        quantize(0)
+        warm = ps.tile([P, P], F32, tag="b0")
+        for warm_pass in range(WARM_PASSES):
+            nc.tensor.matmul_mx(
+                out=warm[:],
+                lhsT=wa_codes[0][:, quarter[0]].bitcast(FP8X4),
+                lhsT_scale=wa_plane[0][:, quarter[0]],
+                rhs=wa_codes[0][:, quarter[0]].bitcast(FP8X4),
+                rhs_scale=wa_plane[0][:, quarter[0]],
+                start=True,
+                stop=True,
+            )
+        for j in range(TILES):
+            wa_pass(a_ps[j], 0, j, quarter[0], start=True)
+
+        eb = sb.tile([P, TILES], F32)
+        eb_eps = sb.tile([P, TILES], F32)
+        ea = sb.tile([P, TILES], F32)
+        den = sb.tile([P, TILES], F32)
+        inv = sb.tile([P, TILES], F32)
+
+        b_ps = []
+        for j in range(TILES):
+            tokens = slice(j * P, (j + 1) * P)
+            bank = ps.tile([P, N], F32, name="b%d" % j, tag="b%d" % j)
+            for z in range(2):
+                nc.tensor.matmul_mx(
+                    out=bank[:],
+                    lhsT=xt[:, z, tokens].bitcast(FP8X4),
+                    lhsT_scale=xt_plane[:, z, tokens],
+                    rhs=wc[:, z, :].bitcast(FP4X4),
+                    rhs_scale=wc_plane[:, z, :],
+                    start=(z == 0),
+                    stop=(z == 1),
+                )
+            b_ps.append(bank)
+
+        def energy(bank, total, cols=whole):
+            squares = sb.tile([P, N], F32, bufs=2)
+            nc.scalar.activation(
+                out=squares[:, cols], in_=bank[:, cols], func=ACT.Square, scale=N**-0.5, accum_out=total
+            )
+
+        weighed = {}
+        for j in range(TILES):
+            energy(b_ps[j], eb[:, j : j + 1])
+            if j > 1:
+                weighed[j - 1] = sb.tile([P, N], F32, name="weighed%d" % (j - 1))
+                nc.scalar.activation(
+                    out=weighed[j - 1][:], in_=b_ps[j - 1][:], func=ACT.Copy, scale=eb[:, j - 1 : j]
+                )
+        nc.scalar.activation(out=eb_eps[:], in_=eb[:], func=ACT.Copy, bias=EPS)
+
+        a0_right = ps.tile([P, N], F32, tag="b1")
+        for i in (1, 2):
+            cast(i)
+            quantize(i)
+        cast(3)
+        for i in (4, 5):
+            cast(i)
+            quantize(i - 1)
+        quantize(5)
+
         for j in range(TILES):
             wa_pass(a_ps[j], 0, j, quarter[1])
             if j > 0:
                 wa_pass(a_ps[j], 0, j, right)
         wa_pass(a0_right, 0, 0, right, start=True)
-        wa_pass(a_ps[0], 1, 0, left)
+        for j in range(TILES):
+            wa_pass(a_ps[j], 1, j, left)
         wa_pass(a0_right, 1, 0, quarter[2])
-        ws_pass(a_ps[0], 0, quarter[0], False)
-        ws_pass(a_ps[0], 0, quarter[1], True)
-        ws_pass(a0_right, 0, quarter[2], False)
-        ws_pass(a0_right, 0, quarter[3], False)
+        ws_pass(a_ps[0], 0, quarter[0])
+        ws_pass(a_ps[0], 0, quarter[1], stop=True)
+        ws_pass(a0_right, 0, quarter[2])
+        ws_pass(a0_right, 0, quarter[3])
         wa_pass(a0_right, 1, 0, quarter[3], stop=True)
         for j in range(1, TILES):
-            wa_pass(a_ps[j], 1, j, whole)
-            ws_pass(a_ps[j], j, whole, True)
+            wa_pass(a_ps[j], 1, j, right)
+            ws_pass(a_ps[j], j, whole, stop=True)
 
         left_sums = sb.tile([P, 2], F32)
         right_sum = sb.tile([P, 1], F32)
-        first = sb.tile([P, 2], F32)
-        bg = sb.tile([P, N], F32)
-        ag = sb.tile([P, N], F32)
-        v = sb.tile([P, N], F32)
+        ea_den0 = sb.tile([P, 2], F32)
+        b_gm = sb.tile([P, N], F32)
+        a_gm = sb.tile([P, N], F32)
+        mixed_gm = sb.tile([P, N], F32)
         nc.vector.scalar_tensor_tensor(
-            out=bg[:], in0=b_ps[0][:], scalar=eb[:, 0:1], in1=gm_all[:], op0=ALU.mult, op1=ALU.mult
+            out=b_gm[:], in0=b_ps[0][:], scalar=eb[:, 0:1], in1=gm_all[:], op0=ALU.mult, op1=ALU.mult
         )
-        be[3] = sb.tile([P, N], F32, name="be3")
-        nc.vector.tensor_scalar(out=be[3][:], in0=b_ps[3][:], scalar1=eb[:, 3:4], scalar2=None, op0=ALU.mult)
+        weighed[LAST] = sb.tile([P, N], F32, name="weighed%d" % LAST)
+        nc.vector.tensor_scalar(
+            out=weighed[LAST][:], in0=b_ps[LAST][:], scalar1=eb[:, LAST:], scalar2=None, op0=ALU.mult
+        )
         energy(a_ps[0], left_sums[:, 0:1], left)
         energy(a0_right, right_sum[:], right)
-        nc.scalar.activation(out=left_sums[:, 1:2], in_=left_sums[:, 0:1], func=ACT.Identity, bias=ebe[:, 0:1])
-        nc.scalar.activation(out=first[:], in_=left_sums[:], func=ACT.Identity, bias=right_sum[:])
+        nc.scalar.activation(out=left_sums[:, 1:2], in_=left_sums[:, 0:1], func=ACT.Identity, bias=eb_eps[:, 0:1])
+        nc.scalar.activation(out=ea_den0[:], in_=left_sums[:], func=ACT.Identity, bias=right_sum[:])
         for bank, cols in ((a_ps[0], left), (a0_right, right)):
-            nc.vector.tensor_tensor(out=ag[:, cols], in0=bank[:, cols], in1=gm_all[:, cols], op=ALU.mult)
+            nc.vector.tensor_tensor(out=a_gm[:, cols], in0=bank[:, cols], in1=gm_all[:, cols], op=ALU.mult)
         for cols in (left, right):
             nc.vector.scalar_tensor_tensor(
-                out=v[:, cols], in0=ag[:, cols], scalar=first[:, 0:1], in1=bg[:, cols], op0=ALU.mult, op1=ALU.add
+                out=mixed_gm[:, cols],
+                in0=a_gm[:, cols],
+                scalar=ea_den0[:, 0:1],
+                in1=b_gm[:, cols],
+                op0=ALU.mult,
+                op1=ALU.add,
             )
-        nc.vector.reciprocal(out=inv[:, 0:1], in_=first[:, 1:2])
+        nc.vector.reciprocal(out=inv[:, 0:1], in_=ea_den0[:, 1:2])
         y0 = sb.tile([P, N], F32)
-        nc.gpsimd.tensor_scalar(out=y0[:], in0=v[:], scalar1=inv[:, 0:1], scalar2=0.0, op0=ALU.mult, op1=ALU.add)
+        nc.gpsimd.tensor_scalar(out=y0[:], in0=mixed_gm[:], scalar1=inv[:, 0:1], scalar2=0.0, op0=ALU.mult, op1=ALU.add)
         nc.sync.dma_start(out=out[0:P, :], in_=y0[:])
 
         mixed = {}
 
-        def denominator(j):
+        def invert_denominator(j):
             col = slice(j, j + 1)
-            nc.scalar.activation(out=den[:, col], in_=ea[:, col], func=ACT.Identity, bias=ebe[:, col])
-
-        def invert(j):
-            nc.vector.reciprocal(out=inv[:, j : j + 1], in_=den[:, j : j + 1])
+            nc.scalar.activation(out=den[:, col], in_=ea[:, col], func=ACT.Identity, bias=eb_eps[:, col])
+            nc.vector.reciprocal(out=inv[:, col], in_=den[:, col])
 
         def mix(j):
             mixed[j] = sb.tile([P, N], F32, name="mixed%d" % j)
             nc.vector.scalar_tensor_tensor(
-                out=mixed[j][:], in0=a_ps[j][:], scalar=ea[:, j : j + 1], in1=be[j][:], op0=ALU.mult, op1=ALU.add
+                out=mixed[j][:], in0=a_ps[j][:], scalar=ea[:, j : j + 1], in1=weighed[j][:], op0=ALU.mult, op1=ALU.add
             )
 
         def finish(j, cols):
             y = sb.tile([P, cols.stop - cols.start], F32, name="y%d_%d" % (j, cols.start))
             nc.vector.scalar_tensor_tensor(
-                out=y[:], in0=mixed[j][:, cols], scalar=inv[:, j : j + 1], in1=gm_all[:, cols], op0=ALU.mult, op1=ALU.mult
+                out=y[:],
+                in0=mixed[j][:, cols],
+                scalar=inv[:, j : j + 1],
+                in1=gm_all[:, cols],
+                op0=ALU.mult,
+                op1=ALU.mult,
             )
             nc.sync.dma_start(out=out[j * P : (j + 1) * P, cols], in_=y[:])
 
-        for j in range(1, TILES):
+        energy(a_ps[1], ea[:, 1:2])
+        mix(1)
+        for j in range(2, TILES):
             energy(a_ps[j], ea[:, j : j + 1])
-            if j > 1:
-                denominator(j - 1)
-                invert(j - 1)
+            invert_denominator(j - 1)
             mix(j)
-            if j == TILES - 1:
-                denominator(j)
-                invert(j)
-            if j > 1:
-                finish(j - 1, whole)
-        finish(TILES - 1, left)
-        finish(TILES - 1, right)
+            if j == LAST:
+                invert_denominator(LAST)
+            finish(j - 1, whole)
+        finish(LAST, left)
+        finish(LAST, right)

from contextlib import ExitStack

import concourse.mybir as mybir
from concourse.masks import make_identity

K, L, T, N = 1024, 512, 512, 512
FLOPS = 2 * T * N * (2 * K + L)

F32 = mybir.dt.float32
BF16 = mybir.dt.bfloat16
I32 = mybir.dt.int32
U32 = mybir.dt.uint32
U8 = mybir.dt.uint8
FP8X4 = mybir.dt.float8_e4m3fn_x4
FP4X4 = mybir.dt.float4_e2m1fn_x4
ALU = mybir.AluOpType
ACT = mybir.ActivationFunctionType

P = 128
PACK = 4
K_PASS = P * PACK
TILES = T // P
LAST = TILES - 1
EPS = 0.01
SCALE_ROWS = 4
WA_PIECES = [(0, 0, 128), (0, 128, 128), (0, 256, 256), (1, 0, 256), (1, 256, 128), (1, 384, 128)]
WARM_PASSES = 6


def tile_mix_rows_mixed_by_their_energy_kernel(
    tc, xt_words, xt_scales, wa, xs_words, xs_scales, ws_words, ws_scales, wc_words, wc_scales, gm, out
):
    nc = tc.nc
    left, right, whole = slice(0, N // 2), slice(N // 2, N), slice(0, N)
    quarter = [slice(q * P, (q + 1) * P) for q in range(N // P)]

    with ExitStack() as ctx:
        sb = ctx.enter_context(tc.tile_pool(name="sb", bufs=1))
        ps = ctx.enter_context(tc.psum_pool(name="ps", bufs=1))
        ctx.enter_context(tc.manual_schedule())

        xt_plane = sb.tile([P, 2, T], U8, align_bytes=64)
        wc_plane = sb.tile([P, 2, N], U8, align_bytes=64)
        ws_plane = sb.tile([P, 1, N], U8, align_bytes=64)
        xs_plane = sb.tile([P, 1, T], U8, align_bytes=64)
        for plane in (xt_plane, wc_plane, xs_plane, ws_plane):
            nc.vector.memset(plane[:].bitcast(I32), 0)

        gm_rows = sb.tile([P, PACK], F32)
        ident = sb.tile([P, P], F32)
        make_identity(nc, ident[:])

        xt = sb.tile([P, 2, T], U32, align_bytes=64)
        wc = sb.tile([P, 2, 2 * N], U8, align_bytes=64)
        xs = sb.tile([P, 2 * T], U8, align_bytes=64)
        ws = sb.tile([P, N], U32, align_bytes=64)

        def load_scales(queue, plane, scales, rows=range(SCALE_ROWS)):
            for r in rows:
                queue.dma_start(
                    out=plane[r:P:32, :, :].bitcast(I32),
                    in_=scales[:, r : 4 * SCALE_ROWS : SCALE_ROWS, :].rearrange("z q c -> q z c").bitcast(I32),
                )

        raw = []

        def load_wa(i):
            z, c0, w = WA_PIECES[i]
            piece = sb.tile([P, PACK, w], F32, name="raw%d" % i)
            rows = wa[K_PASS * z : K_PASS * (z + 1), c0 : c0 + w]
            nc.sync.dma_start(out=piece[:], in_=rows.rearrange("(p j) c -> p j c", j=PACK))
            raw.append(piece)

        load_wa(0)
        load_scales(nc.sync, xt_plane, xt_scales)
        nc.sync.dma_start(out=gm_rows[:], in_=gm.rearrange("o (p c) -> (o p) c", c=PACK))
        nc.sync.dma_start(out=xt[:].bitcast(I32), in_=xt_words.rearrange("z p c r -> p z (c r)").bitcast(I32))
        nc.sync.dma_start(out=wc[:].bitcast(I32), in_=wc_words.rearrange("z p c -> p z c").bitcast(I32))
        load_scales(nc.sync, wc_plane, wc_scales)
        load_scales(nc.gpsimd, xs_plane, xs_scales)
        load_wa(1)
        load_wa(2)
        load_scales(nc.sync, ws_plane, ws_scales, range(1))
        load_wa(3)
        load_wa(4)
        nc.sync.dma_start(out=xs[:].bitcast(I32), in_=xs_words[0].bitcast(I32))
        load_wa(5)
        load_scales(nc.sync, ws_plane, ws_scales, range(1, SCALE_ROWS))
        nc.sync.dma_start(out=ws[:].bitcast(I32), in_=ws_words[0].rearrange("p c r -> p (c r)").bitcast(I32))

        gm_ps = ps.tile([P, PACK, P], F32, tag="b%d" % LAST)
        for c in range(PACK):
            nc.tensor.transpose(gm_ps[:, c, :], gm_rows[:, c : c + 1].to_broadcast([P, P]), ident[:])
        gm_all = sb.tile([P, N], F32)
        nc.scalar.copy(out=gm_all[:].rearrange("p (m c) -> p m c", c=PACK), in_=gm_ps[:].rearrange("p c m -> p m c"))

        a_ps = [ps.tile([P, N], F32, name="a%d" % j, tag="a%d" % j) for j in range(TILES)]
        wa_codes = [sb.tile([P, N], U32, name="wa_codes%d" % z, align_bytes=64) for z in range(2)]
        wa_plane = [sb.tile([P, N], U8, name="wa_plane%d" % z, align_bytes=64) for z in range(2)]
        grouped = []

        def cast(i):
            piece = sb.tile([P, WA_PIECES[i][2], PACK], BF16, name="grouped%d" % i, align_bytes=64)
            nc.vector.tensor_copy(
                out=piece[:].rearrange("p (c i) j -> p c j i", i=4),
                in_=raw[i][:].rearrange("p j (c i) -> p c j i", i=4),
            )
            grouped.append(piece)

        def quantize(i):
            z, c0, w = WA_PIECES[i]
            nc.vector.quantize_mx(
                out=wa_codes[z][:, c0 : c0 + w].bitcast(FP8X4),
                scales=wa_plane[z][:, c0 : c0 + w],
                in_=grouped[i][:].rearrange("p w j -> p (w j)"),
            )

        def wa_pass(bank, z, j, cols, start=False, stop=False):
            tokens = slice(j * P, (j + 1) * P)
            nc.tensor.matmul_mx(
                out=bank[:, cols],
                lhsT=xt[:, z, tokens].bitcast(FP8X4),
                lhsT_scale=xt_plane[:, z, tokens],
                rhs=wa_codes[z][:, cols].bitcast(FP8X4),
                rhs_scale=wa_plane[z][:, cols],
                start=start,
                stop=stop,
            )

        def ws_pass(bank, j, cols, stop=False):
            nc.tensor.matmul_mx(
                out=bank[:, cols],
                lhsT=xs[:, 2 * j * P : 2 * (j + 1) * P].bitcast(FP4X4),
                lhsT_scale=xs_plane[:, 0, j * P : (j + 1) * P],
                rhs=ws[:, cols].bitcast(FP8X4),
                rhs_scale=ws_plane[:, 0, cols],
                start=False,
                stop=stop,
            )

        cast(0)
        quantize(0)
        warm = ps.tile([P, P], F32, tag="b0")
        for warm_pass in range(WARM_PASSES):
            nc.tensor.matmul_mx(
                out=warm[:],
                lhsT=wa_codes[0][:, quarter[0]].bitcast(FP8X4),
                lhsT_scale=wa_plane[0][:, quarter[0]],
                rhs=wa_codes[0][:, quarter[0]].bitcast(FP8X4),
                rhs_scale=wa_plane[0][:, quarter[0]],
                start=True,
                stop=True,
            )
        for j in range(TILES):
            wa_pass(a_ps[j], 0, j, quarter[0], start=True)

        eb = sb.tile([P, TILES], F32)
        eb_eps = sb.tile([P, TILES], F32)
        ea = sb.tile([P, TILES], F32)
        den = sb.tile([P, TILES], F32)
        inv = sb.tile([P, TILES], F32)

        b_ps = []
        for j in range(TILES):
            tokens = slice(j * P, (j + 1) * P)
            bank = ps.tile([P, N], F32, name="b%d" % j, tag="b%d" % j)
            for z in range(2):
                nc.tensor.matmul_mx(
                    out=bank[:],
                    lhsT=xt[:, z, tokens].bitcast(FP8X4),
                    lhsT_scale=xt_plane[:, z, tokens],
                    rhs=wc[:, z, :].bitcast(FP4X4),
                    rhs_scale=wc_plane[:, z, :],
                    start=(z == 0),
                    stop=(z == 1),
                )
            b_ps.append(bank)

        def energy(bank, total, cols=whole):
            squares = sb.tile([P, N], F32, bufs=2)
            nc.scalar.activation(
                out=squares[:, cols], in_=bank[:, cols], func=ACT.Square, scale=N**-0.5, accum_out=total
            )

        weighed = {}
        for j in range(TILES):
            energy(b_ps[j], eb[:, j : j + 1])
            if j > 1:
                weighed[j - 1] = sb.tile([P, N], F32, name="weighed%d" % (j - 1))
                nc.scalar.activation(
                    out=weighed[j - 1][:], in_=b_ps[j - 1][:], func=ACT.Copy, scale=eb[:, j - 1 : j]
                )
        nc.scalar.activation(out=eb_eps[:], in_=eb[:], func=ACT.Copy, bias=EPS)

        a0_right = ps.tile([P, N], F32, tag="b1")
        for i in (1, 2):
            cast(i)
            quantize(i)
        cast(3)
        for i in (4, 5):
            cast(i)
            quantize(i - 1)
        quantize(5)

        for j in range(TILES):
            wa_pass(a_ps[j], 0, j, quarter[1])
            if j > 0:
                wa_pass(a_ps[j], 0, j, right)
        wa_pass(a0_right, 0, 0, right, start=True)
        for j in range(TILES):
            wa_pass(a_ps[j], 1, j, left)
        wa_pass(a0_right, 1, 0, quarter[2])
        ws_pass(a_ps[0], 0, quarter[0])
        ws_pass(a_ps[0], 0, quarter[1], stop=True)
        ws_pass(a0_right, 0, quarter[2])
        ws_pass(a0_right, 0, quarter[3])
        wa_pass(a0_right, 1, 0, quarter[3], stop=True)
        for j in range(1, TILES):
            wa_pass(a_ps[j], 1, j, right)
            ws_pass(a_ps[j], j, whole, stop=True)

        left_sums = sb.tile([P, 2], F32)
        right_sum = sb.tile([P, 1], F32)
        ea_den0 = sb.tile([P, 2], F32)
        b_gm = sb.tile([P, N], F32)
        a_gm = sb.tile([P, N], F32)
        mixed_gm = sb.tile([P, N], F32)
        nc.vector.scalar_tensor_tensor(
            out=b_gm[:], in0=b_ps[0][:], scalar=eb[:, 0:1], in1=gm_all[:], op0=ALU.mult, op1=ALU.mult
        )
        weighed[LAST] = sb.tile([P, N], F32, name="weighed%d" % LAST)
        nc.vector.tensor_scalar(
            out=weighed[LAST][:], in0=b_ps[LAST][:], scalar1=eb[:, LAST:], scalar2=None, op0=ALU.mult
        )
        energy(a_ps[0], left_sums[:, 0:1], left)
        energy(a0_right, right_sum[:], right)
        nc.scalar.activation(out=left_sums[:, 1:2], in_=left_sums[:, 0:1], func=ACT.Identity, bias=eb_eps[:, 0:1])
        nc.scalar.activation(out=ea_den0[:], in_=left_sums[:], func=ACT.Identity, bias=right_sum[:])
        for bank, cols in ((a_ps[0], left), (a0_right, right)):
            nc.vector.tensor_tensor(out=a_gm[:, cols], in0=bank[:, cols], in1=gm_all[:, cols], op=ALU.mult)
        for cols in (left, right):
            nc.vector.scalar_tensor_tensor(
                out=mixed_gm[:, cols],
                in0=a_gm[:, cols],
                scalar=ea_den0[:, 0:1],
                in1=b_gm[:, cols],
                op0=ALU.mult,
                op1=ALU.add,
            )
        nc.vector.reciprocal(out=inv[:, 0:1], in_=ea_den0[:, 1:2])
        y0 = sb.tile([P, N], F32)
        nc.gpsimd.tensor_scalar(out=y0[:], in0=mixed_gm[:], scalar1=inv[:, 0:1], scalar2=0.0, op0=ALU.mult, op1=ALU.add)
        nc.sync.dma_start(out=out[0:P, :], in_=y0[:])

        mixed = {}

        def invert_denominator(j):
            col = slice(j, j + 1)
            nc.scalar.activation(out=den[:, col], in_=ea[:, col], func=ACT.Identity, bias=eb_eps[:, col])
            nc.vector.reciprocal(out=inv[:, col], in_=den[:, col])

        def mix(j):
            mixed[j] = sb.tile([P, N], F32, name="mixed%d" % j)
            nc.vector.scalar_tensor_tensor(
                out=mixed[j][:], in0=a_ps[j][:], scalar=ea[:, j : j + 1], in1=weighed[j][:], op0=ALU.mult, op1=ALU.add
            )

        def finish(j, cols):
            y = sb.tile([P, cols.stop - cols.start], F32, name="y%d_%d" % (j, cols.start))
            nc.vector.scalar_tensor_tensor(
                out=y[:],
                in0=mixed[j][:, cols],
                scalar=inv[:, j : j + 1],
                in1=gm_all[:, cols],
                op0=ALU.mult,
                op1=ALU.mult,
            )
            nc.sync.dma_start(out=out[j * P : (j + 1) * P, cols], in_=y[:])

        energy(a_ps[1], ea[:, 1:2])
        mix(1)
        for j in range(2, TILES):
            energy(a_ps[j], ea[:, j : j + 1])
            invert_denominator(j - 1)
            mix(j)
            if j == LAST:
                invert_denominator(LAST)
            finish(j - 1, whole)
        finish(LAST, left)
        finish(LAST, right)
